import numpy as np
import ml_dtypes


def mxq(x, axis, fmt="e4m3"):
    dtype, down = {"e4m3": (ml_dtypes.float8_e4m3fn, 7), "e5m2": (ml_dtypes.float8_e5m2, 14)}[fmt]
    v = np.moveaxis(np.asarray(x, np.float32).astype(ml_dtypes.bfloat16).astype(np.float64), axis, -1)
    blocks = v.reshape(v.shape[:-1] + (-1, 32))
    amax = np.abs(blocks).max(-1, keepdims=True)
    byte = np.maximum(np.where(amax > 0, np.frexp(amax)[1] - 1 + 127, 0) - down, 1)
    scale = np.exp2(byte - 127.0)
    codes = (blocks / scale).astype(np.float32).astype(dtype).astype(np.float64)
    return np.moveaxis((codes * scale).reshape(v.shape), -1, axis)


WIDE = False


def mx_kscale(k):
    if not WIDE:
        return np.ones(k)
    levels = np.array([10, -10, 5, -5, 0])
    if k % 512:
        return np.exp2(np.random.permutation(np.resize(levels, k // 32))).repeat(32)
    a = np.empty((k // 512, 16))
    for p in range(k // 512):
        a[p, :8] = np.random.permutation(np.resize(levels, 8))
        for g in range(8):
            far = levels[np.abs(levels - a[p, g]) >= 10]
            a[p, g + 8] = far[np.random.randint(len(far))]
    return np.exp2(a.ravel()).repeat(32)


def f64(x):
    return np.asarray(x).astype(np.float64)


def striped(idx):
    return np.tile(idx.reshape(-1, 16).T, (8, 1)).astype(np.uint16)


def unstriped(offs):
    return offs[:16].T.reshape(-1).astype(np.int64)


def striped8(idx):
    return np.concatenate([x.reshape(-1, 16).T for x in idx]).astype(np.uint16)


def runs(offs, k):
    lists = np.stack([offs[16 * r : 16 * r + 16].T.reshape(-1) for r in range(8)]).astype(np.int64)
    return lists[np.arange(k) % 512 // 64]


def pack_weight(w):
    k, n = w.shape
    w = f64(np.asarray(w, np.float32).astype(ml_dtypes.bfloat16)).reshape(k // 32, 32, n)
    amax = np.abs(w).max(1)
    byte = np.clip(np.where(amax > 0, np.frexp(amax)[1] - 1 + 127 - 7, 1), 1, 254)
    scaled = (w * np.exp2(127.0 - byte)[:, None, :]).reshape(k, n).astype(np.float32)
    words = np.ascontiguousarray(scaled.reshape(k // 512, 128, 4, n).transpose(0, 1, 3, 2)).astype(ml_dtypes.float8_e4m3fn).view(np.uint8)
    return words, np.ascontiguousarray(byte.astype(np.uint8).reshape(k // 512, 16, n))


def unpack_weight(words, scales):
    g, p, n, _ = words.shape
    vals = np.ascontiguousarray(words).view(ml_dtypes.float8_e4m3fn).astype(np.float64) * np.repeat(np.exp2(scales.astype(np.float64) - 127.0), 8, axis=1)[..., None]
    return vals.transpose(0, 1, 3, 2).reshape(g * 512, n)


K, T, S, H, C = 512, 2048, 512, 512, 512


def setup_inputs():
    n = np.random.standard_normal
    s = mx_kscale(K)[:, None]
    packed_xT = pack_weight(n((K, T)) * s)
    return {
        "x_words": packed_xT[0],
        "x_scales": packed_xT[1],
        "w1": (n((K, H)) / np.sqrt(K) / s).astype(np.float32),
        "gs": (np.random.uniform(0.5, 1.5, (K, 1)) / s).astype(np.float32),
        "offs": striped(np.random.permutation(T)[:S]),
        "n1": striped8(np.stack([np.random.permutation(S) for _ in range(8)])),
        "n2": striped8(np.stack([np.random.permutation(S) for _ in range(8)])),
        "n3": striped8(np.stack([np.random.permutation(S) for _ in range(8)])),
        "ca": striped(np.random.permutation(T)[:C]),
        "cb": striped(np.random.permutation(T)[:C]),
        "n4": striped8(np.stack([np.random.permutation(S) for _ in range(8)])),
        "n5": striped8(np.stack([np.random.permutation(S) for _ in range(8)])),
    }


def reference(x_words, x_scales, w1, gs, offs, n1, n2, n3, ca, cb, n4, n5):
    x_ca = unpack_weight(x_words, x_scales)[:, unstriped(ca)]
    xq = unpack_weight(x_words, x_scales)[:, unstriped(offs)]
    y = mxq(f64(w1), 0, "e4m3").T @ xq
    b1 = y[np.arange(H)[:, None], runs(n1, H)]
    b2 = y[np.arange(H)[:, None], runs(n2, H)]
    b3 = y[np.arange(H)[:, None], runs(n3, H)]
    z = f64(gs) * (np.maximum(np.maximum(b1, b2), b3) - (0.5 * (np.maximum(np.minimum(b1, b2), np.minimum(np.maximum(b1, b2), b3)))))
    zq = mxq(z, 0, "e4m3")
    a = 0.0625 * (x_ca.T @ zq)
    x_cb = unpack_weight(x_words, x_scales)[:, unstriped(cb)]
    b = 0.0625 * (x_cb.T @ zq)
    return a[np.arange(C)[:, None], runs(n4, C)] - (np.tanh(b) * (b[np.arange(C)[:, None], runs(n5, C)]))

@@ -1,0 +1,196 @@
+from contextlib import ExitStack
+
+import concourse.mybir as mybir
+
+F32 = mybir.dt.float32
+BF16 = mybir.dt.bfloat16
+I32 = mybir.dt.int32
+U32 = mybir.dt.uint32
+U16 = mybir.dt.uint16
+U8 = mybir.dt.uint8
+FP8X4 = mybir.dt.float8_e4m3fn_x4
+ALU = mybir.AluOpType
+ACT = mybir.ActivationFunctionType
+
+P = 128
+PACK = 4
+T = 2048
+S = 512
+FLOPS = 3 * 2 * 512 * 512 * 512
+Z_CHUNKS = ((0, 256), (256, 128), (384, 128))
+OUT_CHUNKS = ((0, 256), (256, 256))
+
+
+def entries(lst, start, count):
+    return lst[:, start // 16 : (start + count) // 16]
+
+
+def tile_picked_ccmpsoftbtop2_none_p_kernel(
+    tc, x_words, x_scales, w1, gs, offs, n1, n2, n3, ca, cb, n4, n5, out
+):
+    nc = tc.nc
+    with ExitStack() as ctx:
+        keep = ctx.enter_context(tc.tile_pool(name="keep", bufs=1))
+        psum = ctx.enter_context(tc.psum_pool(name="psum", bufs=1))
+
+        def load_list(name, src):
+            lst = keep.tile([P, S // 16], U16, name=name)
+            nc.sync.dma_start(lst[:], src)
+            return lst
+
+        warm = keep.tile([P, 8], F32, name="warm")
+        nc.gpsimd.memset(warm[:], 0.0)
+        warm_out = keep.tile([P, 8], F32, name="warm_out")
+        nc.scalar.activation(warm_out[:], warm[:], ACT.Tanh)
+
+        table_scales = keep.tile([P, T], U8, name="table_scales")
+        nc.vector.memset(table_scales[:].bitcast(I32), 0)
+        l_offs = load_list("l_offs", offs)
+        for q in range(4):
+            nc.sync.dma_start(
+                table_scales[32 * q : 32 * q + 4, :].bitcast(I32),
+                x_scales[0, 4 * q : 4 * q + 4, :].bitcast(I32),
+            )
+        w_view = w1.rearrange("(p j) c -> p j c", j=PACK)
+        w_raw = [keep.tile([P, PACK, 256], F32, name="w_raw%d" % h) for h in range(2)]
+        nc.sync.dma_start(w_raw[0][:], w_view[:, :, 0:256])
+        l_cb = load_list("l_cb", cb)
+        nc.sync.dma_start(w_raw[1][:], w_view[:, :, 256:512])
+        l_ca = load_list("l_ca", ca)
+        table_words = keep.tile([P, T], I32, name="table_words")
+        nc.sync.dma_start(table_words[:], x_words[0].rearrange("p n r -> p (n r)").bitcast(I32))
+        l_n1 = load_list("l_n1", n1)
+        l_n2 = load_list("l_n2", n2)
+        l_n3 = load_list("l_n3", n3)
+        gs_sb = keep.tile([P, PACK], F32, name="gs_sb")
+        nc.sync.dma_start(gs_sb[:], gs.rearrange("(p t) o -> p (t o)", t=PACK))
+        l_n5 = load_list("l_n5", n5)
+        l_n4 = load_list("l_n4", n4)
+
+        words_window = table_words[:].bitcast(U32)
+
+        xq_scales = keep.tile([P, S], U8, name="xq_scales", align_bytes=64)
+        nc.vector.tensor_copy(xq_scales[:], table_scales[:].indirect(l_offs[:]))
+        pair_raw = keep.tile([P, 2 * S], U8, name="pair_raw", align_bytes=64)
+        nc.vector.tensor_copy(pair_raw[:, 0:S], table_scales[:].indirect(l_cb[:]))
+        nc.vector.tensor_copy(pair_raw[:, S : 2 * S], table_scales[:].indirect(l_ca[:]))
+
+        w_bf = keep.tile([P, PACK, P, PACK], BF16, name="w_bf", align_bytes=64)
+        for h in range(2):
+            nc.scalar.copy(
+                w_bf[:, :, 64 * h : 64 * h + 64, :].rearrange("p t m j -> p m j t"),
+                w_raw[h][:].rearrange("p j (m t) -> p m j t", t=PACK),
+            )
+        w_codes = keep.tile([P, S], U32, name="w_codes", align_bytes=64)
+        w_scales = keep.tile([P, S], U8, name="w_scales", align_bytes=64)
+        nc.vector.quantize_mx(w_codes[:].bitcast(FP8X4), w_scales[:], w_bf[:].rearrange("p t m j -> p (t m j)"))
+
+        xq_words = keep.tile([P, S], U32, name="xq_words", align_bytes=64)
+        nc.vector.tensor_copy(xq_words[:], words_window.indirect(l_offs[:]))
+
+        pair_scales = keep.tile([P, 2 * S], U8, name="pair_scales", align_bytes=64)
+        nc.vector.tensor_copy(
+            pair_scales[:].rearrange("p (l t m) -> p l t m", l=2, t=PACK),
+            pair_raw[:].rearrange("p (l m t) -> p l t m", l=2, t=PACK),
+        )
+        cb_words = keep.tile([P, S], U32, name="cb_words", align_bytes=64)
+        nc.vector.tensor_copy(
+            cb_words[:].rearrange("p (t m) -> p m t", t=PACK), words_window.indirect(l_cb[:])
+        )
+
+        half_y = []
+        for t in range(PACK):
+            bank = psum.tile([P, S], F32, name="ya%d" % t)
+            cols = slice(P * t, P * (t + 1))
+            nc.tensor.matmul_mx(
+                bank[:], w_codes[:, cols].bitcast(FP8X4), w_scales[:, cols],
+                xq_words[:].bitcast(FP8X4), xq_scales[:], start=True, stop=True,
+            )
+            hy = keep.tile([P, S], F32, name="half_y%d" % t)
+            nc.scalar.activation(hy[:], bank[:], ACT.Copy, scale=0.5)
+            half_y.append(hy)
+
+        z_codes = keep.tile([P, S], U32, name="z_codes", align_bytes=64)
+        z_scales = keep.tile([P, S], U8, name="z_scales", align_bytes=64)
+        b_banks = [psum.tile([P, S], F32, name="b%d" % t) for t in range(PACK)]
+        b_rows = [keep.tile([P, S], F32, name="b_rows%d" % t) for t in range(PACK)]
+        b_tanh = [keep.tile([P, S], F32, name="b_tanh%d" % t) for t in range(PACK)]
+
+        for c, (j0, n) in enumerate(Z_CHUNKS):
+            def planes(name, dtype=F32):
+                return keep.tile([P, PACK, n], dtype, name="%s%d" % (name, c), align_bytes=64)
+
+            h1, d, hi, gap, e, low, top, hs = [planes(s) for s in ("h1", "d", "hi", "gap", "e", "low", "top", "hs")]
+            z_planes = planes("z_planes", BF16)
+            for t in range(PACK):
+                nc.vector.tensor_copy(h1[:, t, :], half_y[t][:].indirect(entries(l_n1, j0, n)))
+            for t in range(PACK):
+                nc.vector.tensor_tensor(d[:, t, :], half_y[t][:].indirect(entries(l_n2, j0, n)), h1[:, t, :], ALU.subtract)
+            pairs = [slice(0, 2), slice(2, 4)]
+            for u in pairs:
+                nc.scalar.activation(gap[:, u, :], d[:, u, :], ACT.Abs)
+                nc.vector.scalar_tensor_tensor(hi[:, u, :], d[:, u, :], 0.0, h1[:, u, :], ALU.max, ALU.add)
+            for t in range(PACK):
+                nc.scalar.activation(hs[:, t, :], hi[:, t, :], ACT.Copy, scale=gs_sb[:, t : t + 1])
+                nc.vector.tensor_tensor(e[:, t, :], half_y[t][:].indirect(entries(l_n3, j0, n)), hi[:, t, :], ALU.subtract)
+            for u in pairs:
+                nc.vector.scalar_tensor_tensor(low[:, u, :], e[:, u, :], -1.0, gap[:, u, :], ALU.mult, ALU.min)
+            for u in pairs:
+                nc.vector.scalar_tensor_tensor(top[:, u, :], e[:, u, :], 2.0, low[:, u, :], ALU.mult, ALU.max)
+            for t in range(PACK):
+                nc.vector.scalar_tensor_tensor(
+                    z_planes[:, t, :], top[:, t, :], gs_sb[:, t : t + 1], hs[:, t, :], ALU.mult, ALU.add
+                )
+            z_bf = keep.tile([P, n, PACK], BF16, name="z_bf%d" % c, align_bytes=64)
+            nc.scalar.copy(
+                z_bf[:].rearrange("p (c i) t -> p c t i", i=4),
+                z_planes[:].rearrange("p t (c i) -> p c t i", i=4),
+            )
+            js = slice(j0, j0 + n)
+            nc.vector.quantize_mx(z_codes[:, js].bitcast(FP8X4), z_scales[:, js], z_bf[:].rearrange("p n t -> p (n t)"))
+            for t in range(PACK):
+                cols = slice(P * t, P * (t + 1))
+                nc.tensor.matmul_mx(
+                    b_banks[t][:, js], cb_words[:, cols].bitcast(FP8X4), pair_scales[:, cols],
+                    z_codes[:, js].bitcast(FP8X4), z_scales[:, js], start=True, stop=True,
+                )
+                nc.scalar.activation(b_rows[t][:, js], b_banks[t][:, js], ACT.Copy, scale=0.0625)
+            for t in range(PACK):
+                nc.scalar.activation(b_tanh[t][:, js], b_banks[t][:, js], ACT.Tanh, scale=0.0625)
+
+        ca_words = keep.tile([P, S], U32, name="top%d" % (len(Z_CHUNKS) - 1), align_bytes=64)
+        nc.vector.tensor_copy(
+            ca_words[:].rearrange("p (t m) -> p m t", t=PACK), words_window.indirect(l_ca[:])
+        )
+        a_rows = []
+        for t in range(PACK):
+            bank = psum.tile([P, S], F32, name="ya%d" % t)
+            cols = slice(P * t, P * (t + 1))
+            nc.tensor.matmul_mx(
+                bank[:], ca_words[:, cols].bitcast(FP8X4), pair_scales[:, S + P * t : S + P * (t + 1)],
+                z_codes[:].bitcast(FP8X4), z_scales[:], start=True, stop=True,
+            )
+            rows = keep.tile([P, S], F32, name="a_rows%d" % t)
+            nc.scalar.activation(rows[:], bank[:], ACT.Copy, scale=0.0625)
+            a_rows.append(rows)
+
+        out_view = out.rearrange("(p t) j -> p t j", t=PACK)
+        prod = [keep.tile([P, S], F32, name="prod%d" % t) for t in range(PACK)]
+        res = [keep.tile([P, S], F32, name="res%d" % t) for t in range(PACK)]
+
+        def product(t):
+            for j0, n in OUT_CHUNKS:
+                js = slice(j0, j0 + n)
+                nc.vector.tensor_tensor(prod[t][:, js], b_rows[t][:].indirect(entries(l_n5, j0, n)), b_tanh[t][:, js], ALU.mult)
+
+        def result(t):
+            for j0, n in OUT_CHUNKS:
+                js = slice(j0, j0 + n)
+                nc.vector.tensor_tensor(res[t][:, js], a_rows[t][:].indirect(entries(l_n4, j0, n)), prod[t][:, js], ALU.subtract)
+                nc.sync.dma_start(out_view[:, t, js], res[t][:, js])
+
+        product(0)
+        for t in range(1, PACK):
+            product(t)
+            result(t - 1)
+        result(PACK - 1)

@@ -1,6 +1,7 @@
 from contextlib import ExitStack
 
 import concourse.mybir as mybir
+from concourse.masks import make_identity
 
 F32 = mybir.dt.float32
 BF16 = mybir.dt.bfloat16
@@ -17,7 +18,7 @@ PACK = 4
 T = 2048
 S = 512
 FLOPS = 3 * 2 * 512 * 512 * 512
-Z_CHUNKS = ((0, 256), (256, 128), (384, 128))
+HALF = 256
 OUT_CHUNKS = ((0, 256), (256, 256))
 
 
@@ -38,13 +39,16 @@ def tile_picked_ccmpsoftbtop2_none_p_kernel(
             nc.sync.dma_start(lst[:], src)
             return lst
 
+        table_scales = keep.tile([P, T], U8, name="table_scales")
+        nc.gpsimd.memset(table_scales[:].bitcast(I32), 0)
         warm = keep.tile([P, 8], F32, name="warm")
         nc.gpsimd.memset(warm[:], 0.0)
         warm_out = keep.tile([P, 8], F32, name="warm_out")
         nc.scalar.activation(warm_out[:], warm[:], ACT.Tanh)
 
-        table_scales = keep.tile([P, T], U8, name="table_scales")
-        nc.vector.memset(table_scales[:].bitcast(I32), 0)
+        ident = keep.tile([P, P], F32, name="ident")
+        make_identity(nc, ident[:])
+
         l_offs = load_list("l_offs", offs)
         for q in range(4):
             nc.sync.dma_start(
@@ -86,111 +90,190 @@ def tile_picked_ccmpsoftbtop2_none_p_kernel(
         nc.vector.quantize_mx(w_codes[:].bitcast(FP8X4), w_scales[:], w_bf[:].rearrange("p t m j -> p (t m j)"))
 
         xq_words = keep.tile([P, S], U32, name="xq_words", align_bytes=64)
-        nc.vector.tensor_copy(xq_words[:], words_window.indirect(l_offs[:]))
+        for j0 in (0, HALF):
+            nc.vector.tensor_copy(xq_words[:, j0 : j0 + HALF], words_window.indirect(entries(l_offs, j0, HALF)))
 
         pair_scales = keep.tile([P, 2 * S], U8, name="pair_scales", align_bytes=64)
         nc.vector.tensor_copy(
-            pair_scales[:].rearrange("p (l t m) -> p l t m", l=2, t=PACK),
-            pair_raw[:].rearrange("p (l m t) -> p l t m", l=2, t=PACK),
+            pair_scales[:].bitcast(I32).rearrange("p (l t g r) -> p l t g r", l=2, t=PACK, g=16),
+            pair_raw[:].bitcast(I32).rearrange("p (l g t r) -> p l t g r", l=2, t=PACK, g=16),
         )
         cb_words = keep.tile([P, S], U32, name="cb_words", align_bytes=64)
         nc.vector.tensor_copy(
-            cb_words[:].rearrange("p (t m) -> p m t", t=PACK), words_window.indirect(l_cb[:])
+            cb_words[:].rearrange("p (t g r) -> p g t r", t=PACK, g=16), words_window.indirect(l_cb[:])
         )
 
-        half_y = []
-        for t in range(PACK):
-            bank = psum.tile([P, S], F32, name="ya%d" % t)
-            cols = slice(P * t, P * (t + 1))
-            nc.tensor.matmul_mx(
-                bank[:], w_codes[:, cols].bitcast(FP8X4), w_scales[:, cols],
-                xq_words[:].bitcast(FP8X4), xq_scales[:], start=True, stop=True,
-            )
-            hy = keep.tile([P, S], F32, name="half_y%d" % t)
-            nc.scalar.activation(hy[:], bank[:], ACT.Copy, scale=0.5)
-            half_y.append(hy)
+        half_y = [keep.tile([P, S], F32, name="half_y%d" % t) for t in range(PACK)]
+        neg_y = [keep.tile([P, S], F32, name="neg_y%d" % t) for t in range(PACK)]
+        y_banks = [psum.tile([P, S], F32, name="ya%d" % t) for t in range(PACK)]
+        for j0 in (0, HALF):
+            js = slice(j0, j0 + HALF)
+            for t in range(PACK):
+                cols = slice(P * t, P * (t + 1))
+                nc.tensor.matmul_mx(
+                    y_banks[t][:, js], w_codes[:, cols].bitcast(FP8X4), w_scales[:, cols],
+                    xq_words[:, js].bitcast(FP8X4), xq_scales[:, js], start=True, stop=True,
+                )
+                if t < 2:
+                    nc.scalar.activation(half_y[t][:, js], y_banks[t][:, js], ACT.Copy, scale=0.5)
+
+        def y_out(rows, u, scale):
+            for t in (2 * u, 2 * u + 1):
+                nc.scalar.activation(rows[t][:], y_banks[t][:], ACT.Copy, scale=scale)
+
+        y_out(neg_y, 0, -0.5)
 
         z_codes = keep.tile([P, S], U32, name="z_codes", align_bytes=64)
         z_scales = keep.tile([P, S], U8, name="z_scales", align_bytes=64)
         b_banks = [psum.tile([P, S], F32, name="b%d" % t) for t in range(PACK)]
-        b_rows = [keep.tile([P, S], F32, name="b_rows%d" % t) for t in range(PACK)]
+        b_rows = [keep.tile([P, 2 * S], F32, name="b_rows%d" % t, align_bytes=64) for t in range(PACK)]
+        a_rows = [keep.tile([P, 2 * S], F32, name="a_rows%d" % t, align_bytes=64) for t in range(PACK)]
         b_tanh = [keep.tile([P, S], F32, name="b_tanh%d" % t) for t in range(PACK)]
 
-        for c, (j0, n) in enumerate(Z_CHUNKS):
-            def planes(name, dtype=F32):
-                return keep.tile([P, PACK, n], dtype, name="%s%d" % (name, c), align_bytes=64)
+        n = HALF
+        z_planes = [keep.tile([P, 2, PACK, P], BF16, name="z_planes%d" % c, align_bytes=64) for c in range(2)]
 
-            h1, d, hi, gap, e, low, top, hs = [planes(s) for s in ("h1", "d", "hi", "gap", "e", "low", "top", "hs")]
-            z_planes = planes("z_planes", BF16)
-            for t in range(PACK):
-                nc.vector.tensor_copy(h1[:, t, :], half_y[t][:].indirect(entries(l_n1, j0, n)))
-            for t in range(PACK):
-                nc.vector.tensor_tensor(d[:, t, :], half_y[t][:].indirect(entries(l_n2, j0, n)), h1[:, t, :], ALU.subtract)
-            pairs = [slice(0, 2), slice(2, 4)]
-            for u in pairs:
-                nc.scalar.activation(gap[:, u, :], d[:, u, :], ACT.Abs)
-                nc.vector.scalar_tensor_tensor(hi[:, u, :], d[:, u, :], 0.0, h1[:, u, :], ALU.max, ALU.add)
-            for t in range(PACK):
-                nc.scalar.activation(hs[:, t, :], hi[:, t, :], ACT.Copy, scale=gs_sb[:, t : t + 1])
-                nc.vector.tensor_tensor(e[:, t, :], half_y[t][:].indirect(entries(l_n3, j0, n)), hi[:, t, :], ALU.subtract)
-            for u in pairs:
-                nc.vector.scalar_tensor_tensor(low[:, u, :], e[:, u, :], -1.0, gap[:, u, :], ALU.mult, ALU.min)
-            for u in pairs:
-                nc.vector.scalar_tensor_tensor(top[:, u, :], e[:, u, :], 2.0, low[:, u, :], ALU.mult, ALU.max)
-            for t in range(PACK):
-                nc.vector.scalar_tensor_tensor(
-                    z_planes[:, t, :], top[:, t, :], gs_sb[:, t : t + 1], hs[:, t, :], ALU.mult, ALU.add
-                )
-            z_bf = keep.tile([P, n, PACK], BF16, name="z_bf%d" % c, align_bytes=64)
+        def pair_tile(name):
+            return keep.tile([P, 2, n], F32, name=name, align_bytes=64)
+
+        def weave(j0, width):
+            c, off = divmod(j0, n)
+            z_bf = keep.tile([P, width, PACK], BF16, name="z_bf%d" % j0, align_bytes=64)
             nc.scalar.copy(
-                z_bf[:].rearrange("p (c i) t -> p c t i", i=4),
-                z_planes[:].rearrange("p t (c i) -> p c t i", i=4),
+                z_bf[:].rearrange("p (h c i) t -> p h c t i", i=4, c=P // 4),
+                z_planes[c][:, off // P : (off + width) // P].rearrange("p h t (c i) -> p h c t i", i=4),
             )
-            js = slice(j0, j0 + n)
-            nc.vector.quantize_mx(z_codes[:, js].bitcast(FP8X4), z_scales[:, js], z_bf[:].rearrange("p n t -> p (n t)"))
-            for t in range(PACK):
-                cols = slice(P * t, P * (t + 1))
-                nc.tensor.matmul_mx(
-                    b_banks[t][:, js], cb_words[:, cols].bitcast(FP8X4), pair_scales[:, cols],
-                    z_codes[:, js].bitcast(FP8X4), z_scales[:, js], start=True, stop=True,
-                )
-                nc.scalar.activation(b_rows[t][:, js], b_banks[t][:, js], ACT.Copy, scale=0.0625)
-            for t in range(PACK):
-                nc.scalar.activation(b_tanh[t][:, js], b_banks[t][:, js], ACT.Tanh, scale=0.0625)
+            return z_bf
 
-        ca_words = keep.tile([P, S], U32, name="top%d" % (len(Z_CHUNKS) - 1), align_bytes=64)
+        def quantize(z_bf, j0, width):
+            js = slice(j0, j0 + width)
+            nc.vector.quantize_mx(z_codes[:, js].bitcast(FP8X4), z_scales[:, js], z_bf[:].rearrange("p n t -> p (n t)"))
+
+        def score_b(t, j0, width, bank):
+            js = slice(j0, j0 + width)
+            cols = slice(P * t, P * (t + 1))
+            nc.tensor.matmul_mx(
+                bank[:, js], cb_words[:, cols].bitcast(FP8X4), pair_scales[:, cols],
+                z_codes[:, js].bitcast(FP8X4), z_scales[:, js], start=True, stop=True,
+            )
+            nc.scalar.activation(b_rows[t][:, js], bank[:, js], ACT.Copy, scale=0.0625)
+
+        def tanh_b(t, j0, width):
+            js = slice(j0, j0 + width)
+            nc.scalar.activation(b_tanh[t][:, js], b_rows[t][:, js], ACT.Tanh)
+
+        for unit in range(4):
+            c, u = divmod(unit, 2)
+            j0 = c * n
+            ts = (2 * u, 2 * u + 1)
+            e, top = [pair_tile("%s%d" % (s, unit)) for s in ("e", "top")]
+            d = a_rows[unit][:, S:].rearrange("p (i n) -> p i n", i=2)
+            low = b_rows[unit][:, S:].rearrange("p (i n) -> p i n", i=2)
+            h1 = [keep.tile([P, n], F32, name="gap%d_%d" % (unit, i)) for i in range(2)]
+            gap = [keep.tile([P, n], F32, name="gap%d_%d" % (unit + 1, i)) for i in range(2)]
+            hi = pair_tile("z_bf0" if unit == 3 else "hi")
+            for i, t in enumerate(ts):
+                nc.vector.tensor_copy(h1[i][:], half_y[t][:].indirect(entries(l_n1, j0, n)))
+            for i, t in enumerate(ts):
+                nc.vector.tensor_tensor(d[:, i, :], half_y[t][:].indirect(entries(l_n2, j0, n)), h1[i][:], ALU.subtract)
+            for i in range(2):
+                nc.scalar.activation(gap[i][:], d[:, i, :], ACT.Abs)
+            if unit == 0:
+                y_out(half_y, 1, 0.5)
+                y_out(neg_y, 1, -0.5)
+            for i in range(2):
+                nc.vector.scalar_tensor_tensor(hi[:, i, :], d[:, i, :], 0.0, h1[i][:], ALU.max, ALU.add)
+            for i, t in enumerate(ts):
+                nc.vector.tensor_tensor(e[:, i, :], neg_y[t][:].indirect(entries(l_n3, j0, n)), hi[:, i, :], ALU.add)
+            for i in range(2):
+                nc.vector.scalar_tensor_tensor(low[:, i, :], e[:, i, :], 0.0, gap[i][:], ALU.max, ALU.min)
+            if unit < 3:
+                nc.scalar.activation(top[:], e[:], ACT.Relu, scale=-2.0)
+                terms = [x[:].rearrange("p t n -> p (t n)") for x in (hi, top)] + [b_rows[unit][:, S:]]
+                turned_bank = psum.tile([P, S], F32, name="ya%d" % (2 * unit % PACK))
+                for blk in range(PACK):
+                    cols = slice(P * blk, P * (blk + 1))
+                    for i, term in enumerate(terms):
+                        nc.tensor.matmul(
+                            turned_bank[:, cols], term[:, cols], ident[:],
+                            start=(i == 0), stop=(i == len(terms) - 1), is_transpose=True,
+                        )
+                turned = keep.tile([P, S], F32, name="turned%d" % unit, align_bytes=64)
+                nc.scalar.copy(turned[:], turned_bank[:])
+                back_bank = psum.tile([P, S], F32, name="ya%d" % ((2 * unit + 1) % PACK))
+                for blk in range(PACK):
+                    cols = slice(P * blk, P * (blk + 1))
+                    nc.tensor.transpose(back_bank[:, cols], turned[:, cols], ident[:])
+                for i, t in enumerate(ts):
+                    nc.scalar.activation(
+                        z_planes[c][:, :, t, :], back_bank[:, n * i : n * (i + 1)].rearrange("p (h j) -> p h j", h=2), ACT.Copy, scale=gs_sb[:, t : t + 1]
+                    )
+                if unit == 1:
+                    quantize(weave(0, n), 0, n)
+                    for t in range(PACK):
+                        score_b(t, 0, n, b_banks[t])
+                    tanh_b(0, 0, n)
+            else:
+                hs = pair_tile("hs")
+                for i, t in enumerate(ts):
+                    nc.scalar.activation(hs[:, i, :], hi[:, i, :], ACT.Copy, scale=gs_sb[:, t : t + 1])
+                for i in range(2):
+                    nc.vector.scalar_tensor_tensor(top[:, i, :], e[:, i, :], -2.0, low[:, i, :], ALU.mult, ALU.max)
+                woven = []
+                for off in (0, P):
+                    for i, t in enumerate(ts):
+                        nc.vector.scalar_tensor_tensor(
+                            z_planes[c][:, off // P, t, :], top[:, i, off : off + P], gs_sb[:, t : t + 1],
+                            hs[:, i, off : off + P], ALU.mult, ALU.add,
+                        )
+                    woven.append(weave(j0 + off, P))
+                side_bank = psum.tile([P, S], F32, name="ya2")
+                for z_bf, off, bank in zip(woven, (0, P), (side_bank, b_banks[0])):
+                    quantize(z_bf, j0 + off, P)
+                    score_b(0, j0 + off, P, bank)
+        tanh_b(0, n, n)
+
+        ca_words = keep.tile([P, S], U32, name="top3", align_bytes=64)
         nc.vector.tensor_copy(
-            ca_words[:].rearrange("p (t m) -> p m t", t=PACK), words_window.indirect(l_ca[:])
+            ca_words[:].rearrange("p (t g r) -> p g t r", t=PACK, g=16), words_window.indirect(l_ca[:])
         )
-        a_rows = []
-        for t in range(PACK):
+
+        def score_a(t):
             bank = psum.tile([P, S], F32, name="ya%d" % t)
             cols = slice(P * t, P * (t + 1))
             nc.tensor.matmul_mx(
                 bank[:], ca_words[:, cols].bitcast(FP8X4), pair_scales[:, S + P * t : S + P * (t + 1)],
                 z_codes[:].bitcast(FP8X4), z_scales[:], start=True, stop=True,
             )
-            rows = keep.tile([P, S], F32, name="a_rows%d" % t)
-            nc.scalar.activation(rows[:], bank[:], ACT.Copy, scale=0.0625)
-            a_rows.append(rows)
+            nc.scalar.activation(a_rows[t][:, 0:S], bank[:], ACT.Copy, scale=0.0625)
 
-        out_view = out.rearrange("(p t) j -> p t j", t=PACK)
+        score_a(0)
+        for t in range(1, PACK):
+            score_b(t, n, n, b_banks[t])
+            tanh_b(t, 0, S)
+            if t > 1:
+                score_a(t - 1)
+        score_a(PACK - 1)
+
+        out_view = out.rearrange("(g t r) j -> t g r j", t=PACK, g=16)
         prod = [keep.tile([P, S], F32, name="prod%d" % t) for t in range(PACK)]
         res = [keep.tile([P, S], F32, name="res%d" % t) for t in range(PACK)]
 
         def product(t):
-            for j0, n in OUT_CHUNKS:
+            for j0, n in OUT_CHUNKS if t == 0 else ((0, S),):
                 js = slice(j0, j0 + n)
                 nc.vector.tensor_tensor(prod[t][:, js], b_rows[t][:].indirect(entries(l_n5, j0, n)), b_tanh[t][:, js], ALU.mult)
 
         def result(t):
-            for j0, n in OUT_CHUNKS:
+            for j0, n in OUT_CHUNKS if t in (0, PACK - 1) else ((0, S),):
                 js = slice(j0, j0 + n)
                 nc.vector.tensor_tensor(res[t][:, js], a_rows[t][:].indirect(entries(l_n4, j0, n)), prod[t][:, js], ALU.subtract)
-                nc.sync.dma_start(out_view[:, t, js], res[t][:, js])
+                nc.sync.dma_start(out_view[t, :, :, js], res[t][:, js])
 
         product(0)
-        for t in range(1, PACK):
+        result(0)
+        product(1)
+        for t in range(2, PACK):
             product(t)
             result(t - 1)
         result(PACK - 1)

@@ -40,7 +40,7 @@ def tile_picked_ccmpsoftbtop2_none_p_kernel(
             return lst
 
         table_scales = keep.tile([P, T], U8, name="table_scales")
-        nc.gpsimd.memset(table_scales[:].bitcast(I32), 0)
+        nc.vector.memset(table_scales[:].bitcast(I32), 0)
         warm = keep.tile([P, 8], F32, name="warm")
         nc.gpsimd.memset(warm[:], 0.0)
         warm_out = keep.tile([P, 8], F32, name="warm_out")
@@ -50,6 +50,7 @@ def tile_picked_ccmpsoftbtop2_none_p_kernel(
         make_identity(nc, ident[:])
 
         l_offs = load_list("l_offs", offs)
+        l_cb = load_list("l_cb", cb)
         for q in range(4):
             nc.sync.dma_start(
                 table_scales[32 * q : 32 * q + 4, :].bitcast(I32),
@@ -58,7 +59,6 @@ def tile_picked_ccmpsoftbtop2_none_p_kernel(
         w_view = w1.rearrange("(p j) c -> p j c", j=PACK)
         w_raw = [keep.tile([P, PACK, 256], F32, name="w_raw%d" % h) for h in range(2)]
         nc.sync.dma_start(w_raw[0][:], w_view[:, :, 0:256])
-        l_cb = load_list("l_cb", cb)
         nc.sync.dma_start(w_raw[1][:], w_view[:, :, 256:512])
         l_ca = load_list("l_ca", ca)
         table_words = keep.tile([P, T], I32, name="table_words")
@@ -106,22 +106,30 @@ def tile_picked_ccmpsoftbtop2_none_p_kernel(
         half_y = [keep.tile([P, S], F32, name="half_y%d" % t) for t in range(PACK)]
         neg_y = [keep.tile([P, S], F32, name="neg_y%d" % t) for t in range(PACK)]
         y_banks = [psum.tile([P, S], F32, name="ya%d" % t) for t in range(PACK)]
-        for j0 in (0, HALF):
-            js = slice(j0, j0 + HALF)
-            for t in range(PACK):
-                cols = slice(P * t, P * (t + 1))
-                nc.tensor.matmul_mx(
-                    y_banks[t][:, js], w_codes[:, cols].bitcast(FP8X4), w_scales[:, cols],
-                    xq_words[:, js].bitcast(FP8X4), xq_scales[:, js], start=True, stop=True,
-                )
-                if t < 2:
-                    nc.scalar.activation(half_y[t][:, js], y_banks[t][:, js], ACT.Copy, scale=0.5)
+        late_banks = [psum.tile([P, S], F32, name="b%d" % t) for t in range(2)]
+
+        def project(bank, t, js):
+            cols = slice(P * t, P * (t + 1))
+            nc.tensor.matmul_mx(
+                bank[:, js], w_codes[:, cols].bitcast(FP8X4), w_scales[:, cols],
+                xq_words[:, js].bitcast(FP8X4), xq_scales[:, js], start=True, stop=True,
+            )
+
+        halves = (slice(0, HALF), slice(HALF, S))
+        for banks, js in zip((y_banks, late_banks), halves):
+            for t in range(2):
+                project(banks[t], t, js)
+                nc.scalar.activation(half_y[t][:, js], banks[t][:, js], ACT.Copy, scale=0.5)
+        for t in range(2, PACK):
+            project(y_banks[t], t, slice(0, S))
+        for t in range(2):
+            nc.scalar.activation(neg_y[t][:], half_y[t][:], ACT.Copy, scale=-1.0)
 
         def y_out(rows, u, scale):
             for t in (2 * u, 2 * u + 1):
                 nc.scalar.activation(rows[t][:], y_banks[t][:], ACT.Copy, scale=scale)
 
-        y_out(neg_y, 0, -0.5)
+        y_out(half_y, 1, 0.5)
 
         z_codes = keep.tile([P, S], U32, name="z_codes", align_bytes=64)
         z_scales = keep.tile([P, S], U8, name="z_scales", align_bytes=64)
@@ -136,10 +144,10 @@ def tile_picked_ccmpsoftbtop2_none_p_kernel(
         def pair_tile(name):
             return keep.tile([P, 2, n], F32, name=name, align_bytes=64)
 
-        def weave(j0, width):
+        def weave(j0, width, copy):
             c, off = divmod(j0, n)
             z_bf = keep.tile([P, width, PACK], BF16, name="z_bf%d" % j0, align_bytes=64)
-            nc.scalar.copy(
+            copy(
                 z_bf[:].rearrange("p (h c i) t -> p h c t i", i=4, c=P // 4),
                 z_planes[c][:, off // P : (off + width) // P].rearrange("p h t (c i) -> p h c t i", i=4),
             )
@@ -157,10 +165,11 @@ def tile_picked_ccmpsoftbtop2_none_p_kernel(
                 z_codes[:, js].bitcast(FP8X4), z_scales[:, js], start=True, stop=True,
             )
             nc.scalar.activation(b_rows[t][:, js], bank[:, js], ACT.Copy, scale=0.0625)
+            return bank[:, js]
 
-        def tanh_b(t, j0, width):
-            js = slice(j0, j0 + width)
-            nc.scalar.activation(b_tanh[t][:, js], b_rows[t][:, js], ACT.Tanh)
+        def tanh_b(t, j0, width, sums):
+            nc.scalar.activation(b_tanh[t][:, j0 : j0 + width], sums, ACT.Tanh, scale=0.0625)
+
 
         for unit in range(4):
             c, u = divmod(unit, 2)
@@ -171,16 +180,13 @@ def tile_picked_ccmpsoftbtop2_none_p_kernel(
             low = b_rows[unit][:, S:].rearrange("p (i n) -> p i n", i=2)
             h1 = [keep.tile([P, n], F32, name="gap%d_%d" % (unit, i)) for i in range(2)]
             gap = [keep.tile([P, n], F32, name="gap%d_%d" % (unit + 1, i)) for i in range(2)]
-            hi = pair_tile("z_bf0" if unit == 3 else "hi")
+            hi = pair_tile("hi%d" % unit)
             for i, t in enumerate(ts):
                 nc.vector.tensor_copy(h1[i][:], half_y[t][:].indirect(entries(l_n1, j0, n)))
             for i, t in enumerate(ts):
                 nc.vector.tensor_tensor(d[:, i, :], half_y[t][:].indirect(entries(l_n2, j0, n)), h1[i][:], ALU.subtract)
             for i in range(2):
                 nc.scalar.activation(gap[i][:], d[:, i, :], ACT.Abs)
-            if unit == 0:
-                y_out(half_y, 1, 0.5)
-                y_out(neg_y, 1, -0.5)
             for i in range(2):
                 nc.vector.scalar_tensor_tensor(hi[:, i, :], d[:, i, :], 0.0, h1[i][:], ALU.max, ALU.add)
             for i, t in enumerate(ts):
@@ -189,8 +195,10 @@ def tile_picked_ccmpsoftbtop2_none_p_kernel(
                 nc.vector.scalar_tensor_tensor(low[:, i, :], e[:, i, :], 0.0, gap[i][:], ALU.max, ALU.min)
             if unit < 3:
                 nc.scalar.activation(top[:], e[:], ACT.Relu, scale=-2.0)
-                terms = [x[:].rearrange("p t n -> p (t n)") for x in (hi, top)] + [b_rows[unit][:, S:]]
-                turned_bank = psum.tile([P, S], F32, name="ya%d" % (2 * unit % PACK))
+                if unit == 0:
+                    y_out(neg_y, 1, -0.5)
+                terms = [b_rows[unit][:, S:]] + [x[:].rearrange("p t n -> p (t n)") for x in (hi, top)]
+                turned_bank = psum.tile([P, S], F32, name="ya0")
                 for blk in range(PACK):
                     cols = slice(P * blk, P * (blk + 1))
                     for i, term in enumerate(terms):
@@ -209,31 +217,33 @@ def tile_picked_ccmpsoftbtop2_none_p_kernel(
                         z_planes[c][:, :, t, :], back_bank[:, n * i : n * (i + 1)].rearrange("p (h j) -> p h j", h=2), ACT.Copy, scale=gs_sb[:, t : t + 1]
                     )
                 if unit == 1:
-                    quantize(weave(0, n), 0, n)
-                    for t in range(PACK):
-                        score_b(t, 0, n, b_banks[t])
-                    tanh_b(0, 0, n)
+                    quantize(weave(0, n, nc.scalar.copy), 0, n)
+
+                if unit == 2:
+                    early_bank = psum.tile([P, S], F32, name="ya1")
+                    tanh_b(0, 0, n, score_b(0, 0, n, early_bank))
             else:
                 hs = pair_tile("hs")
                 for i, t in enumerate(ts):
                     nc.scalar.activation(hs[:, i, :], hi[:, i, :], ACT.Copy, scale=gs_sb[:, t : t + 1])
                 for i in range(2):
                     nc.vector.scalar_tensor_tensor(top[:, i, :], e[:, i, :], -2.0, low[:, i, :], ALU.mult, ALU.max)
-                woven = []
                 for off in (0, P):
                     for i, t in enumerate(ts):
                         nc.vector.scalar_tensor_tensor(
                             z_planes[c][:, off // P, t, :], top[:, i, off : off + P], gs_sb[:, t : t + 1],
                             hs[:, i, off : off + P], ALU.mult, ALU.add,
                         )
-                    woven.append(weave(j0 + off, P))
+                woven = [weave(j0 + off, P, nc.vector.tensor_copy) for off in (0, P)]
                 side_bank = psum.tile([P, S], F32, name="ya2")
+                sums = []
                 for z_bf, off, bank in zip(woven, (0, P), (side_bank, b_banks[0])):
                     quantize(z_bf, j0 + off, P)
-                    score_b(0, j0 + off, P, bank)
-        tanh_b(0, n, n)
+                    sums.append(score_b(0, j0 + off, P, bank))
+                for part, off in zip(sums, (0, P)):
+                    tanh_b(0, j0 + off, P, part)
 
-        ca_words = keep.tile([P, S], U32, name="top3", align_bytes=64)
+        ca_words = keep.tile([P, S], U32, name="z_bf256", align_bytes=64)
         nc.vector.tensor_copy(
             ca_words[:].rearrange("p (t g r) -> p g t r", t=PACK, g=16), words_window.indirect(l_ca[:])
         )
@@ -247,12 +257,9 @@ def tile_picked_ccmpsoftbtop2_none_p_kernel(
             )
             nc.scalar.activation(a_rows[t][:, 0:S], bank[:], ACT.Copy, scale=0.0625)
 
-        score_a(0)
         for t in range(1, PACK):
-            score_b(t, n, n, b_banks[t])
-            tanh_b(t, 0, S)
-            if t > 1:
-                score_a(t - 1)
+            tanh_b(t, 0, S, score_b(t, 0, S, b_banks[t]))
+            score_a(t - 1)
         score_a(PACK - 1)
 
         out_view = out.rearrange("(g t r) j -> t g r j", t=PACK, g=16)
@@ -265,15 +272,13 @@ def tile_picked_ccmpsoftbtop2_none_p_kernel(
                 nc.vector.tensor_tensor(prod[t][:, js], b_rows[t][:].indirect(entries(l_n5, j0, n)), b_tanh[t][:, js], ALU.mult)
 
         def result(t):
-            for j0, n in OUT_CHUNKS if t in (0, PACK - 1) else ((0, S),):
+            for j0, n in OUT_CHUNKS if t == PACK - 1 else ((0, S),):
                 js = slice(j0, j0 + n)
                 nc.vector.tensor_tensor(res[t][:, js], a_rows[t][:].indirect(entries(l_n4, j0, n)), prod[t][:, js], ALU.subtract)
                 nc.sync.dma_start(out_view[t, :, :, js], res[t][:, js])
 
         product(0)
-        result(0)
-        product(1)
-        for t in range(2, PACK):
+        for t in range(1, PACK):
             product(t)
             result(t - 1)
         result(PACK - 1)

@@ -104,7 +104,7 @@ def tile_picked_ccmpsoftbtop2_none_p_kernel(
         )
 
         half_y = [keep.tile([P, S], F32, name="half_y%d" % t) for t in range(PACK)]
-        neg_y = [keep.tile([P, S], F32, name="neg_y%d" % t) for t in range(PACK)]
+        neg_y = [keep.tile([P, S], F32, name="neg_y%d" % t) for t in range(2)]
         y_banks = [psum.tile([P, S], F32, name="ya%d" % t) for t in range(PACK)]
         late_banks = [psum.tile([P, S], F32, name="b%d" % t) for t in range(2)]
 
@@ -122,14 +122,7 @@ def tile_picked_ccmpsoftbtop2_none_p_kernel(
                 nc.scalar.activation(half_y[t][:, js], banks[t][:, js], ACT.Copy, scale=0.5)
         for t in range(2, PACK):
             project(y_banks[t], t, slice(0, S))
-        for t in range(2):
-            nc.scalar.activation(neg_y[t][:], half_y[t][:], ACT.Copy, scale=-1.0)
-
-        def y_out(rows, u, scale):
-            for t in (2 * u, 2 * u + 1):
-                nc.scalar.activation(rows[t][:], y_banks[t][:], ACT.Copy, scale=scale)
-
-        y_out(half_y, 1, 0.5)
+            nc.scalar.activation(half_y[t][:], y_banks[t][:], ACT.Copy, scale=0.5)
 
         z_codes = keep.tile([P, S], U32, name="z_codes", align_bytes=64)
         z_scales = keep.tile([P, S], U8, name="z_scales", align_bytes=64)
@@ -171,54 +164,83 @@ def tile_picked_ccmpsoftbtop2_none_p_kernel(
             nc.scalar.activation(b_tanh[t][:, j0 : j0 + width], sums, ACT.Tanh, scale=0.0625)
 
 
+        def turn(bank, sources):
+            for blk in range(PACK):
+                cols = slice(P * blk, P * (blk + 1))
+                for i, src in enumerate(sources):
+                    nc.tensor.matmul(
+                        bank[:, cols], src[:, cols], ident[:],
+                        start=(i == 0), stop=(i == len(sources) - 1), is_transpose=True,
+                    )
+
+        def flat(x):
+            return x[:].rearrange("p i n -> p (i n)")
+
+        neg_gs = keep.tile([P, PACK], F32, name="neg_gs")
+        nc.scalar.activation(neg_gs[:], gs_sb[:], ACT.Copy, scale=-1.0)
+
         for unit in range(4):
             c, u = divmod(unit, 2)
             j0 = c * n
             ts = (2 * u, 2 * u + 1)
-            e, top = [pair_tile("%s%d" % (s, unit)) for s in ("e", "top")]
-            d = a_rows[unit][:, S:].rearrange("p (i n) -> p i n", i=2)
-            low = b_rows[unit][:, S:].rearrange("p (i n) -> p i n", i=2)
-            h1 = [keep.tile([P, n], F32, name="gap%d_%d" % (unit, i)) for i in range(2)]
-            gap = [keep.tile([P, n], F32, name="gap%d_%d" % (unit + 1, i)) for i in range(2)]
-            hi = pair_tile("hi%d" % unit)
+            one_step = unit < 2
+            top = pair_tile("turned%d" % (unit - 1) if unit in (1, 2) else "top%d" % unit)
+            low = pair_tile("low%d" % unit)
+            d = pair_tile("d%d" % unit)
+            hi_flat, e_flat = a_rows[unit][:, S:], b_rows[unit][:, S:]
+            hi = hi_flat.rearrange("p (i n) -> p i n", i=2)
+            e = e_flat.rearrange("p (i n) -> p i n", i=2)
+            h1_pair = pair_tile("clip0" if unit == 3 else "h1")
+            h1 = [h1_pair[:, i, :] for i in range(2)]
+            gap_pair = pair_tile("clip%d" % (unit - 2) if unit >= 2 else "gap%d" % unit)
+            gap = [gap_pair[:, i, :] for i in range(2)]
             for i, t in enumerate(ts):
-                nc.vector.tensor_copy(h1[i][:], half_y[t][:].indirect(entries(l_n1, j0, n)))
+                nc.vector.tensor_copy(h1[i], half_y[t][:].indirect(entries(l_n1, j0, n)))
             for i, t in enumerate(ts):
-                nc.vector.tensor_tensor(d[:, i, :], half_y[t][:].indirect(entries(l_n2, j0, n)), h1[i][:], ALU.subtract)
+                nc.vector.tensor_tensor(d[:, i, :], half_y[t][:].indirect(entries(l_n2, j0, n)), h1[i], ALU.subtract)
+            nc.scalar.activation(flat(gap_pair), flat(d), ACT.Abs)
             for i in range(2):
-                nc.scalar.activation(gap[i][:], d[:, i, :], ACT.Abs)
-            for i in range(2):
-                nc.vector.scalar_tensor_tensor(hi[:, i, :], d[:, i, :], 0.0, h1[i][:], ALU.max, ALU.add)
+                nc.vector.scalar_tensor_tensor(hi[:, i, :], d[:, i, :], 0.0, h1[i], ALU.max, ALU.add)
+            negated = unit < 3 and not one_step
             for i, t in enumerate(ts):
-                nc.vector.tensor_tensor(e[:, i, :], neg_y[t][:].indirect(entries(l_n3, j0, n)), hi[:, i, :], ALU.add)
-            for i in range(2):
-                nc.vector.scalar_tensor_tensor(low[:, i, :], e[:, i, :], 0.0, gap[i][:], ALU.max, ALU.min)
+                if negated:
+                    nc.vector.tensor_tensor(e[:, i, :], neg_y[t][:].indirect(entries(l_n3, j0, n)), hi[:, i, :], ALU.add)
+                else:
+                    nc.vector.tensor_tensor(e[:, i, :], half_y[t][:].indirect(entries(l_n3, j0, n)), hi[:, i, :], ALU.subtract)
             if unit < 3:
-                nc.scalar.activation(top[:], e[:], ACT.Relu, scale=-2.0)
-                if unit == 0:
-                    y_out(neg_y, 1, -0.5)
-                terms = [b_rows[unit][:, S:]] + [x[:].rearrange("p t n -> p (t n)") for x in (hi, top)]
-                turned_bank = psum.tile([P, S], F32, name="ya0")
-                for blk in range(PACK):
-                    cols = slice(P * blk, P * (blk + 1))
-                    for i, term in enumerate(terms):
-                        nc.tensor.matmul(
-                            turned_bank[:, cols], term[:, cols], ident[:],
-                            start=(i == 0), stop=(i == len(terms) - 1), is_transpose=True,
-                        )
-                turned = keep.tile([P, S], F32, name="turned%d" % unit, align_bytes=64)
-                nc.scalar.copy(turned[:], turned_bank[:])
-                back_bank = psum.tile([P, S], F32, name="ya%d" % ((2 * unit + 1) % PACK))
-                for blk in range(PACK):
-                    cols = slice(P * blk, P * (blk + 1))
-                    nc.tensor.transpose(back_bank[:, cols], turned[:, cols], ident[:])
+                back_bank_name = "ya%d" % ((2 * unit + 1) % PACK)
+                if one_step:
+                    nc.scalar.activation(flat(top), e_flat, ACT.Relu, scale=3.0)
+                    clip_bank = psum.tile([P, S], F32, name=("b2", "ya0")[unit])
+                    turn(clip_bank, [e_flat, flat(gap_pair)])
+                    rest_bank = psum.tile([P, S], F32, name=("ya0", "b2")[unit])
+                    turn(rest_bank, [flat(top), hi_flat, flat(gap_pair)])
+                    clip = keep.tile([P, S], F32, name="clip%d" % unit, align_bytes=64)
+                    nc.scalar.activation(clip[:], clip_bank[:], ACT.Relu)
+                    turned = keep.tile([P, S], F32, name="turned%d" % unit, align_bytes=64)
+                    nc.scalar.activation(turned[:], rest_bank[:], ACT.Copy, scale=-1.0)
+                    parts, weight = [turned[:], clip[:]], neg_gs
+                else:
+                    for i in range(2):
+                        nc.vector.scalar_tensor_tensor(low[:, i, :], e[:, i, :], 0.0, gap[i], ALU.max, ALU.min)
+                    nc.scalar.activation(flat(top), e_flat, ACT.Relu, scale=-2.0)
+                    rest_bank = psum.tile([P, S], F32, name="b2")
+                    turn(rest_bank, [flat(low), hi_flat, flat(top)])
+                    turned = keep.tile([P, S], F32, name="turned%d" % unit, align_bytes=64)
+                    nc.scalar.copy(turned[:], rest_bank[:])
+                    parts, weight = [turned[:]], gs_sb
+                back_bank = psum.tile([P, S], F32, name=back_bank_name)
+                turn(back_bank, parts)
                 for i, t in enumerate(ts):
                     nc.scalar.activation(
-                        z_planes[c][:, :, t, :], back_bank[:, n * i : n * (i + 1)].rearrange("p (h j) -> p h j", h=2), ACT.Copy, scale=gs_sb[:, t : t + 1]
+                        z_planes[c][:, :, t, :], back_bank[:, n * i : n * (i + 1)].rearrange("p (h j) -> p h j", h=2),
+                        ACT.Copy, scale=weight[:, t : t + 1],
                     )
+                if unit == 0 and 2 < 3:
+                    for t in range(2):
+                        nc.scalar.activation(neg_y[t][:], half_y[t][:], ACT.Copy, scale=-1.0)
                 if unit == 1:
                     quantize(weave(0, n, nc.scalar.copy), 0, n)
-
                 if unit == 2:
                     early_bank = psum.tile([P, S], F32, name="ya1")
                     tanh_b(0, 0, n, score_b(0, 0, n, early_bank))
@@ -227,7 +249,9 @@ def tile_picked_ccmpsoftbtop2_none_p_kernel(
                 for i, t in enumerate(ts):
                     nc.scalar.activation(hs[:, i, :], hi[:, i, :], ACT.Copy, scale=gs_sb[:, t : t + 1])
                 for i in range(2):
-                    nc.vector.scalar_tensor_tensor(top[:, i, :], e[:, i, :], -2.0, low[:, i, :], ALU.mult, ALU.max)
+                    nc.vector.scalar_tensor_tensor(low[:, i, :], e[:, i, :], -1.0, gap[i], ALU.mult, ALU.min)
+                for i in range(2):
+                    nc.vector.scalar_tensor_tensor(top[:, i, :], e[:, i, :], 2.0, low[:, i, :], ALU.mult, ALU.max)
                 for off in (0, P):
                     for i, t in enumerate(ts):
                         nc.vector.scalar_tensor_tensor(

@@ -17,13 +17,18 @@ P = 128
 PACK = 4
 T = 2048
 S = 512
+HALF = S // 2
+RUNS = 16
+SCORE_SCALE = 0.0625
 FLOPS = 3 * 2 * 512 * 512 * 512
-HALF = 256
-OUT_CHUNKS = ((0, 256), (256, 256))
 
 
 def entries(lst, start, count):
     return lst[:, start // 16 : (start + count) // 16]
+
+
+def flat(pair):
+    return pair.rearrange("p i n -> p (i n)")
 
 
 def tile_picked_ccmpsoftbtop2_none_p_kernel(
@@ -34,6 +39,9 @@ def tile_picked_ccmpsoftbtop2_none_p_kernel(
         keep = ctx.enter_context(tc.tile_pool(name="keep", bufs=1))
         psum = ctx.enter_context(tc.psum_pool(name="psum", bufs=1))
 
+        def bank(index):
+            return psum.tile([P, S], F32, name="bank", tag="bank%d" % index)
+
         def load_list(name, src):
             lst = keep.tile([P, S // 16], U16, name=name)
             nc.sync.dma_start(lst[:], src)
@@ -41,11 +49,6 @@ def tile_picked_ccmpsoftbtop2_none_p_kernel(
 
         table_scales = keep.tile([P, T], U8, name="table_scales")
         nc.vector.memset(table_scales[:].bitcast(I32), 0)
-        warm = keep.tile([P, 8], F32, name="warm")
-        nc.gpsimd.memset(warm[:], 0.0)
-        warm_out = keep.tile([P, 8], F32, name="warm_out")
-        nc.scalar.activation(warm_out[:], warm[:], ACT.Tanh)
-
         ident = keep.tile([P, P], F32, name="ident")
         make_identity(nc, ident[:])
 
@@ -56,10 +59,11 @@ def tile_picked_ccmpsoftbtop2_none_p_kernel(
                 table_scales[32 * q : 32 * q + 4, :].bitcast(I32),
                 x_scales[0, 4 * q : 4 * q + 4, :].bitcast(I32),
             )
+        halves = (slice(0, HALF), slice(HALF, S))
         w_view = w1.rearrange("(p j) c -> p j c", j=PACK)
-        w_raw = [keep.tile([P, PACK, 256], F32, name="w_raw%d" % h) for h in range(2)]
-        nc.sync.dma_start(w_raw[0][:], w_view[:, :, 0:256])
-        nc.sync.dma_start(w_raw[1][:], w_view[:, :, 256:512])
+        w_raw = [keep.tile([P, PACK, HALF], F32, name="w_raw%d" % h) for h in range(2)]
+        for h in range(2):
+            nc.sync.dma_start(w_raw[h][:], w_view[:, :, halves[h]])
         l_ca = load_list("l_ca", ca)
         table_words = keep.tile([P, T], I32, name="table_words")
         nc.sync.dma_start(table_words[:], x_words[0].rearrange("p n r -> p (n r)").bitcast(I32))
@@ -70,19 +74,18 @@ def tile_picked_ccmpsoftbtop2_none_p_kernel(
         nc.sync.dma_start(gs_sb[:], gs.rearrange("(p t) o -> p (t o)", t=PACK))
         l_n5 = load_list("l_n5", n5)
         l_n4 = load_list("l_n4", n4)
-
         words_window = table_words[:].bitcast(U32)
 
         xq_scales = keep.tile([P, S], U8, name="xq_scales", align_bytes=64)
         nc.vector.tensor_copy(xq_scales[:], table_scales[:].indirect(l_offs[:]))
-        pair_raw = keep.tile([P, 2 * S], U8, name="pair_raw", align_bytes=64)
-        nc.vector.tensor_copy(pair_raw[:, 0:S], table_scales[:].indirect(l_cb[:]))
-        nc.vector.tensor_copy(pair_raw[:, S : 2 * S], table_scales[:].indirect(l_ca[:]))
+        listed_scales = keep.tile([P, 2 * S], U8, name="listed_scales", align_bytes=64)
+        nc.vector.tensor_copy(listed_scales[:, 0:S], table_scales[:].indirect(l_cb[:]))
+        nc.vector.tensor_copy(listed_scales[:, S : 2 * S], table_scales[:].indirect(l_ca[:]))
 
         w_bf = keep.tile([P, PACK, P, PACK], BF16, name="w_bf", align_bytes=64)
         for h in range(2):
             nc.scalar.copy(
-                w_bf[:, :, 64 * h : 64 * h + 64, :].rearrange("p t m j -> p m j t"),
+                w_bf[:, :, P // 2 * h : P // 2 * (h + 1), :].rearrange("p t m j -> p m j t"),
                 w_raw[h][:].rearrange("p j (m t) -> p m j t", t=PACK),
             )
         w_codes = keep.tile([P, S], U32, name="w_codes", align_bytes=64)
@@ -95,54 +98,58 @@ def tile_picked_ccmpsoftbtop2_none_p_kernel(
 
         pair_scales = keep.tile([P, 2 * S], U8, name="pair_scales", align_bytes=64)
         nc.vector.tensor_copy(
-            pair_scales[:].bitcast(I32).rearrange("p (l t g r) -> p l t g r", l=2, t=PACK, g=16),
-            pair_raw[:].bitcast(I32).rearrange("p (l g t r) -> p l t g r", l=2, t=PACK, g=16),
+            pair_scales[:].bitcast(I32).rearrange("p (l t g r) -> p l t g r", l=2, t=PACK, g=RUNS),
+            listed_scales[:].bitcast(I32).rearrange("p (l g t r) -> p l t g r", l=2, t=PACK, g=RUNS),
         )
-        cb_words = keep.tile([P, S], U32, name="cb_words", align_bytes=64)
-        nc.vector.tensor_copy(
-            cb_words[:].rearrange("p (t g r) -> p g t r", t=PACK, g=16), words_window.indirect(l_cb[:])
-        )
+        cb_scales, ca_scales = pair_scales[:, 0:S], pair_scales[:, S : 2 * S]
 
-        half_y = [keep.tile([P, S], F32, name="half_y%d" % t) for t in range(PACK)]
-        neg_y = [keep.tile([P, S], F32, name="neg_y%d" % t) for t in range(2)]
-        y_banks = [psum.tile([P, S], F32, name="ya%d" % t) for t in range(PACK)]
-        late_banks = [psum.tile([P, S], F32, name="b%d" % t) for t in range(2)]
-
-        def project(bank, t, js):
-            cols = slice(P * t, P * (t + 1))
-            nc.tensor.matmul_mx(
-                bank[:, js], w_codes[:, cols].bitcast(FP8X4), w_scales[:, cols],
-                xq_words[:, js].bitcast(FP8X4), xq_scales[:, js], start=True, stop=True,
+        def gather_dealt_words(words, lst):
+            nc.vector.tensor_copy(
+                words[:].rearrange("p (t g r) -> p g t r", t=PACK, g=RUNS), words_window.indirect(lst[:])
             )
 
-        halves = (slice(0, HALF), slice(HALF, S))
-        for banks, js in zip((y_banks, late_banks), halves):
+        cb_words = keep.tile([P, S], U32, name="cb_words", align_bytes=64)
+        gather_dealt_words(cb_words, l_cb)
+
+        def product(acc, stationary_words, stationary_scales, t, moving_words, moving_scales):
+            cols = slice(P * t, P * (t + 1))
+            nc.tensor.matmul_mx(
+                acc, stationary_words[:, cols].bitcast(FP8X4), stationary_scales[:, cols],
+                moving_words.bitcast(FP8X4), moving_scales, start=True, stop=True,
+            )
+
+        half_y = [keep.tile([P, S], F32, name="half_y%d" % t) for t in range(PACK)]
+
+        def project(acc, t, js):
+            product(acc[:, js], w_codes, w_scales, t, xq_words[:, js], xq_scales[:, js])
+            nc.scalar.activation(half_y[t][:, js], acc[:, js], ACT.Copy, scale=0.5)
+
+        for first_bank, js in zip((0, PACK), halves):
             for t in range(2):
-                project(banks[t], t, js)
-                nc.scalar.activation(half_y[t][:, js], banks[t][:, js], ACT.Copy, scale=0.5)
+                project(bank(first_bank + t), t, js)
         for t in range(2, PACK):
-            project(y_banks[t], t, slice(0, S))
-            nc.scalar.activation(half_y[t][:], y_banks[t][:], ACT.Copy, scale=0.5)
+            project(bank(t), t, slice(0, S))
 
         z_codes = keep.tile([P, S], U32, name="z_codes", align_bytes=64)
         z_scales = keep.tile([P, S], U8, name="z_scales", align_bytes=64)
-        b_banks = [psum.tile([P, S], F32, name="b%d" % t) for t in range(PACK)]
         b_rows = [keep.tile([P, 2 * S], F32, name="b_rows%d" % t, align_bytes=64) for t in range(PACK)]
         a_rows = [keep.tile([P, 2 * S], F32, name="a_rows%d" % t, align_bytes=64) for t in range(PACK)]
         b_tanh = [keep.tile([P, S], F32, name="b_tanh%d" % t) for t in range(PACK)]
+        z_planes = [
+            keep.tile([P, 2, PACK, P], BF16, name="z_planes", tag="z_planes%d" % c, align_bytes=64) for c in range(2)
+        ]
+        neg_gs = keep.tile([P, PACK], F32, name="neg_gs")
+        nc.scalar.activation(neg_gs[:], gs_sb[:], ACT.Copy, scale=-1.0)
 
-        n = HALF
-        z_planes = [keep.tile([P, 2, PACK, P], BF16, name="z_planes%d" % c, align_bytes=64) for c in range(2)]
-
-        def pair_tile(name):
-            return keep.tile([P, 2, n], F32, name=name, align_bytes=64)
+        def pair_tile(name, tag):
+            return keep.tile([P, 2, HALF], F32, name=name, tag=tag, align_bytes=64)[:]
 
         def weave(j0, width, copy):
-            c, off = divmod(j0, n)
-            z_bf = keep.tile([P, width, PACK], BF16, name="z_bf%d" % j0, align_bytes=64)
+            c, off = divmod(j0, HALF)
+            z_bf = keep.tile([P, width, PACK], BF16, name="z_bf", tag="z_bf%d" % j0, align_bytes=64)
             copy(
-                z_bf[:].rearrange("p (h c i) t -> p h c t i", i=4, c=P // 4),
-                z_planes[c][:, off // P : (off + width) // P].rearrange("p h t (c i) -> p h c t i", i=4),
+                z_bf[:].rearrange("p (s c i) t -> p s c t i", i=4, c=P // 4),
+                z_planes[c][:, off // P : (off + width) // P].rearrange("p s t (c i) -> p s c t i", i=4),
             )
             return z_bf
 
@@ -150,159 +157,155 @@ def tile_picked_ccmpsoftbtop2_none_p_kernel(
             js = slice(j0, j0 + width)
             nc.vector.quantize_mx(z_codes[:, js].bitcast(FP8X4), z_scales[:, js], z_bf[:].rearrange("p n t -> p (n t)"))
 
-        def score_b(t, j0, width, bank):
+        def score_b(acc, t, j0, width):
             js = slice(j0, j0 + width)
-            cols = slice(P * t, P * (t + 1))
-            nc.tensor.matmul_mx(
-                bank[:, js], cb_words[:, cols].bitcast(FP8X4), pair_scales[:, cols],
-                z_codes[:, js].bitcast(FP8X4), z_scales[:, js], start=True, stop=True,
-            )
-            nc.scalar.activation(b_rows[t][:, js], bank[:, js], ACT.Copy, scale=0.0625)
-            return bank[:, js]
+            product(acc[:, js], cb_words, cb_scales, t, z_codes[:, js], z_scales[:, js])
+            nc.scalar.activation(b_rows[t][:, js], acc[:, js], ACT.Copy, scale=SCORE_SCALE)
 
-        def tanh_b(t, j0, width, sums):
-            nc.scalar.activation(b_tanh[t][:, j0 : j0 + width], sums, ACT.Tanh, scale=0.0625)
+        def tanh_b(acc, t, j0, width):
+            js = slice(j0, j0 + width)
+            nc.scalar.activation(b_tanh[t][:, js], acc[:, js], ACT.Tanh, scale=SCORE_SCALE)
 
-
-        def turn(bank, sources):
-            for blk in range(PACK):
+        def add_turned(acc, terms, blocks):
+            for blk in blocks:
                 cols = slice(P * blk, P * (blk + 1))
-                for i, src in enumerate(sources):
+                for i, term in enumerate(terms):
                     nc.tensor.matmul(
-                        bank[:, cols], src[:, cols], ident[:],
-                        start=(i == 0), stop=(i == len(sources) - 1), is_transpose=True,
+                        acc[:, cols], term[:, cols], ident[:],
+                        start=(i == 0), stop=(i == len(terms) - 1), is_transpose=True,
                     )
 
-        def flat(x):
-            return x[:].rearrange("p i n -> p (i n)")
-
-        neg_gs = keep.tile([P, PACK], F32, name="neg_gs")
-        nc.scalar.activation(neg_gs[:], gs_sb[:], ACT.Copy, scale=-1.0)
-
-        for unit in range(4):
-            c, u = divmod(unit, 2)
-            j0 = c * n
-            ts = (2 * u, 2 * u + 1)
-            one_step = unit < 2
-            top = pair_tile("turned%d" % (unit - 1) if unit in (1, 2) else "top%d" % unit)
-            low = pair_tile("low%d" % unit)
-            d = pair_tile("d%d" % unit)
-            hi_flat, e_flat = a_rows[unit][:, S:], b_rows[unit][:, S:]
-            hi = hi_flat.rearrange("p (i n) -> p i n", i=2)
-            e = e_flat.rearrange("p (i n) -> p i n", i=2)
-            h1_pair = pair_tile("clip0" if unit == 3 else "h1")
-            h1 = [h1_pair[:, i, :] for i in range(2)]
-            gap_pair = pair_tile("clip%d" % (unit - 2) if unit >= 2 else "gap%d" % unit)
-            gap = [gap_pair[:, i, :] for i in range(2)]
-            for i, t in enumerate(ts):
-                nc.vector.tensor_copy(h1[i], half_y[t][:].indirect(entries(l_n1, j0, n)))
-            for i, t in enumerate(ts):
-                nc.vector.tensor_tensor(d[:, i, :], half_y[t][:].indirect(entries(l_n2, j0, n)), h1[i], ALU.subtract)
-            nc.scalar.activation(flat(gap_pair), flat(d), ACT.Abs)
+        def look_up(quarter, h1_tag, gap_tag, third, third_op):
+            c, u = divmod(quarter, 2)
+            j0 = c * HALF
+            h1 = pair_tile("h1", h1_tag)
+            d = pair_tile("d", "d%d" % quarter)
+            gap = pair_tile("gap", gap_tag)
+            hi = a_rows[quarter][:, S:].rearrange("p (i n) -> p i n", i=2)
+            e = b_rows[quarter][:, S:].rearrange("p (i n) -> p i n", i=2)
             for i in range(2):
-                nc.vector.scalar_tensor_tensor(hi[:, i, :], d[:, i, :], 0.0, h1[i], ALU.max, ALU.add)
-            negated = unit < 3 and not one_step
-            for i, t in enumerate(ts):
-                if negated:
-                    nc.vector.tensor_tensor(e[:, i, :], neg_y[t][:].indirect(entries(l_n3, j0, n)), hi[:, i, :], ALU.add)
-                else:
-                    nc.vector.tensor_tensor(e[:, i, :], half_y[t][:].indirect(entries(l_n3, j0, n)), hi[:, i, :], ALU.subtract)
-            if unit < 3:
-                back_bank_name = "ya%d" % ((2 * unit + 1) % PACK)
-                if one_step:
-                    nc.scalar.activation(flat(top), e_flat, ACT.Relu, scale=3.0)
-                    clip_bank = psum.tile([P, S], F32, name=("b2", "ya0")[unit])
-                    turn(clip_bank, [e_flat, flat(gap_pair)])
-                    rest_bank = psum.tile([P, S], F32, name=("ya0", "b2")[unit])
-                    turn(rest_bank, [flat(top), hi_flat, flat(gap_pair)])
-                    clip = keep.tile([P, S], F32, name="clip%d" % unit, align_bytes=64)
-                    nc.scalar.activation(clip[:], clip_bank[:], ACT.Relu)
-                    turned = keep.tile([P, S], F32, name="turned%d" % unit, align_bytes=64)
-                    nc.scalar.activation(turned[:], rest_bank[:], ACT.Copy, scale=-1.0)
-                    parts, weight = [turned[:], clip[:]], neg_gs
-                else:
-                    for i in range(2):
-                        nc.vector.scalar_tensor_tensor(low[:, i, :], e[:, i, :], 0.0, gap[i], ALU.max, ALU.min)
-                    nc.scalar.activation(flat(top), e_flat, ACT.Relu, scale=-2.0)
-                    rest_bank = psum.tile([P, S], F32, name="b2")
-                    turn(rest_bank, [flat(low), hi_flat, flat(top)])
-                    turned = keep.tile([P, S], F32, name="turned%d" % unit, align_bytes=64)
-                    nc.scalar.copy(turned[:], rest_bank[:])
-                    parts, weight = [turned[:]], gs_sb
-                back_bank = psum.tile([P, S], F32, name=back_bank_name)
-                turn(back_bank, parts)
-                for i, t in enumerate(ts):
-                    nc.scalar.activation(
-                        z_planes[c][:, :, t, :], back_bank[:, n * i : n * (i + 1)].rearrange("p (h j) -> p h j", h=2),
-                        ACT.Copy, scale=weight[:, t : t + 1],
-                    )
-                if unit == 0 and 2 < 3:
-                    for t in range(2):
-                        nc.scalar.activation(neg_y[t][:], half_y[t][:], ACT.Copy, scale=-1.0)
-                if unit == 1:
-                    quantize(weave(0, n, nc.scalar.copy), 0, n)
-                if unit == 2:
-                    early_bank = psum.tile([P, S], F32, name="ya1")
-                    tanh_b(0, 0, n, score_b(0, 0, n, early_bank))
-            else:
-                hs = pair_tile("hs")
-                for i, t in enumerate(ts):
-                    nc.scalar.activation(hs[:, i, :], hi[:, i, :], ACT.Copy, scale=gs_sb[:, t : t + 1])
-                for i in range(2):
-                    nc.vector.scalar_tensor_tensor(low[:, i, :], e[:, i, :], -1.0, gap[i], ALU.mult, ALU.min)
-                for i in range(2):
-                    nc.vector.scalar_tensor_tensor(top[:, i, :], e[:, i, :], 2.0, low[:, i, :], ALU.mult, ALU.max)
-                for off in (0, P):
-                    for i, t in enumerate(ts):
-                        nc.vector.scalar_tensor_tensor(
-                            z_planes[c][:, off // P, t, :], top[:, i, off : off + P], gs_sb[:, t : t + 1],
-                            hs[:, i, off : off + P], ALU.mult, ALU.add,
-                        )
-                woven = [weave(j0 + off, P, nc.vector.tensor_copy) for off in (0, P)]
-                side_bank = psum.tile([P, S], F32, name="ya2")
-                sums = []
-                for z_bf, off, bank in zip(woven, (0, P), (side_bank, b_banks[0])):
-                    quantize(z_bf, j0 + off, P)
-                    sums.append(score_b(0, j0 + off, P, bank))
-                for part, off in zip(sums, (0, P)):
-                    tanh_b(0, j0 + off, P, part)
+                nc.vector.tensor_copy(h1[:, i, :], half_y[2 * u + i][:].indirect(entries(l_n1, j0, HALF)))
+            for i in range(2):
+                nc.vector.tensor_tensor(
+                    d[:, i, :], half_y[2 * u + i][:].indirect(entries(l_n2, j0, HALF)), h1[:, i, :], ALU.subtract
+                )
+            nc.scalar.activation(flat(gap), flat(d), ACT.Abs)
+            for i in range(2):
+                nc.vector.scalar_tensor_tensor(hi[:, i, :], d[:, i, :], 0.0, h1[:, i, :], ALU.max, ALU.add)
+            for i in range(2):
+                nc.vector.tensor_tensor(
+                    e[:, i, :], third[2 * u + i][:].indirect(entries(l_n3, j0, HALF)), hi[:, i, :], third_op
+                )
+            return hi, gap, e
 
-        ca_words = keep.tile([P, S], U32, name="z_bf256", align_bytes=64)
-        nc.vector.tensor_copy(
-            ca_words[:].rearrange("p (t g r) -> p g t r", t=PACK, g=16), words_window.indirect(l_ca[:])
-        )
+        def sum_into_planes(quarter, terms, sign, others, weight):
+            c, u = divmod(quarter, 2)
+            turned = keep.tile([P, S], F32, name="turned", tag="turned%d" % quarter, align_bytes=64)
+            for i in range(2):
+                acc = bank((0, 7)[i])
+                add_turned(acc, terms, (2 * i, 2 * i + 1))
+                nc.scalar.activation(turned[:, halves[i]], acc[:, halves[i]], ACT.Copy, scale=sign)
+            for i in range(2):
+                t = 2 * u + i
+                acc = bank((1, 3)[i])
+                add_turned(acc, [turned[:]] + others, (2 * i, 2 * i + 1))
+                nc.scalar.activation(
+                    z_planes[c][:, :, t, :], acc[:, halves[i]].rearrange("p (s j) -> p s j", j=P),
+                    ACT.Copy, scale=weight[:, t : t + 1],
+                )
+
+        neg_y = [keep.tile([P, S], F32, name="neg_y%d" % t) for t in range(2)]
+        for quarter in range(2):
+            hi, gap, e = look_up(quarter, "h1", "gap%d" % quarter, half_y, ALU.subtract)
+            rise = pair_tile("rise", "rise")
+            for i in range(2):
+                nc.scalar.activation(rise[:, i, :], e[:, i, :], ACT.Relu, scale=3.0)
+            acc = bank(6)
+            add_turned(acc, [flat(e), flat(gap)], range(PACK))
+            clip = keep.tile([P, S], F32, name="clip%d" % quarter, align_bytes=64)
+            nc.scalar.activation(clip[:], acc[:], ACT.Relu)
+            sum_into_planes(quarter, [flat(rise), flat(hi), flat(gap)], -1.0, [clip[:]], neg_gs)
+            if quarter == 0:
+                for t in range(2):
+                    nc.scalar.activation(neg_y[t][:], half_y[t][:], ACT.Copy, scale=-1.0)
+        quantize(weave(0, HALF, nc.scalar.copy), 0, HALF)
+
+        hi, gap, neg_e = look_up(2, "h1", "gap0", neg_y, ALU.add)
+        low = pair_tile("low", "low2")
+        for i in range(2):
+            nc.vector.scalar_tensor_tensor(low[:, i, :], neg_e[:, i, :], 0.0, gap[:, i, :], ALU.max, ALU.min)
+        rise = pair_tile("rise", "gap1")
+        for i in range(2):
+            nc.scalar.activation(rise[:, i, :], neg_e[:, i, :], ACT.Relu, scale=-2.0)
+        sum_into_planes(2, [flat(low), flat(hi), flat(rise)], 1.0, [], gs_sb)
+        acc = bank(1)
+        score_b(acc, 0, 0, HALF)
+        tanh_b(acc, 0, 0, HALF)
+
+        hi, gap, e = look_up(3, "gap0", "z_planes0", half_y, ALU.subtract)
+        weighted_hi = pair_tile("weighted_hi", "turned2")
+        for i in range(2):
+            nc.scalar.activation(weighted_hi[:, i, :], hi[:, i, :], ACT.Copy, scale=gs_sb[:, 2 + i : 3 + i])
+        low = pair_tile("low", "low3")
+        for i in range(2):
+            nc.vector.scalar_tensor_tensor(low[:, i, :], e[:, i, :], -1.0, gap[:, i, :], ALU.mult, ALU.min)
+        top = pair_tile("top", "top")
+        for i in range(2):
+            nc.vector.scalar_tensor_tensor(top[:, i, :], e[:, i, :], 2.0, low[:, i, :], ALU.mult, ALU.max)
+        for s in range(2):
+            js = slice(P * s, P * (s + 1))
+            for i in range(2):
+                nc.vector.scalar_tensor_tensor(
+                    z_planes[1][:, s, 2 + i, :], top[:, i, js], gs_sb[:, 2 + i : 3 + i], weighted_hi[:, i, js],
+                    ALU.mult, ALU.add,
+                )
+
+        starts = (HALF, HALF + P)
+        woven = [weave(j0, P, nc.vector.tensor_copy) for j0 in starts]
+        accs = [bank(2), bank(PACK)]
+        for z_bf, j0, acc in zip(woven, starts, accs):
+            quantize(z_bf, j0, P)
+            score_b(acc, 0, j0, P)
+        for j0, acc in zip(starts, accs):
+            tanh_b(acc, 0, j0, P)
+
+        ca_words = keep.tile([P, S], U32, name="ca_words", tag="z_bf%d" % HALF, align_bytes=64)
+        gather_dealt_words(ca_words, l_ca)
 
         def score_a(t):
-            bank = psum.tile([P, S], F32, name="ya%d" % t)
-            cols = slice(P * t, P * (t + 1))
-            nc.tensor.matmul_mx(
-                bank[:], ca_words[:, cols].bitcast(FP8X4), pair_scales[:, S + P * t : S + P * (t + 1)],
-                z_codes[:].bitcast(FP8X4), z_scales[:], start=True, stop=True,
-            )
-            nc.scalar.activation(a_rows[t][:, 0:S], bank[:], ACT.Copy, scale=0.0625)
+            acc = bank(t)
+            product(acc[:], ca_words, ca_scales, t, z_codes[:], z_scales[:])
+            nc.scalar.activation(a_rows[t][:, 0:S], acc[:], ACT.Copy, scale=SCORE_SCALE)
 
         for t in range(1, PACK):
-            tanh_b(t, 0, S, score_b(t, 0, S, b_banks[t]))
+            acc = bank(PACK + t)
+            score_b(acc, t, 0, S)
+            tanh_b(acc, t, 0, S)
             score_a(t - 1)
         score_a(PACK - 1)
 
-        out_view = out.rearrange("(g t r) j -> t g r j", t=PACK, g=16)
+        out_view = out.rearrange("(g t r) j -> t g r j", t=PACK, g=RUNS)
         prod = [keep.tile([P, S], F32, name="prod%d" % t) for t in range(PACK)]
         res = [keep.tile([P, S], F32, name="res%d" % t) for t in range(PACK)]
+        whole, halved = ((0, S),), ((0, HALF), (HALF, HALF))
 
-        def product(t):
-            for j0, n in OUT_CHUNKS if t == 0 else ((0, S),):
-                js = slice(j0, j0 + n)
-                nc.vector.tensor_tensor(prod[t][:, js], b_rows[t][:].indirect(entries(l_n5, j0, n)), b_tanh[t][:, js], ALU.mult)
+        def times_tanh(t):
+            for j0, width in halved if t == 0 else whole:
+                js = slice(j0, j0 + width)
+                nc.vector.tensor_tensor(
+                    prod[t][:, js], b_rows[t][:].indirect(entries(l_n5, j0, width)), b_tanh[t][:, js], ALU.mult
+                )
 
         def result(t):
-            for j0, n in OUT_CHUNKS if t == PACK - 1 else ((0, S),):
-                js = slice(j0, j0 + n)
-                nc.vector.tensor_tensor(res[t][:, js], a_rows[t][:].indirect(entries(l_n4, j0, n)), prod[t][:, js], ALU.subtract)
+            for j0, width in halved if t == PACK - 1 else whole:
+                js = slice(j0, j0 + width)
+                nc.vector.tensor_tensor(
+                    res[t][:, js], a_rows[t][:].indirect(entries(l_n4, j0, width)), prod[t][:, js], ALU.subtract
+                )
                 nc.sync.dma_start(out_view[t, :, :, js], res[t][:, js])
 
-        product(0)
+        times_tanh(0)
         for t in range(1, PACK):
-            product(t)
+            times_tanh(t)
             result(t - 1)
         result(PACK - 1)

from contextlib import ExitStack

import concourse.mybir as mybir
from concourse.masks import make_identity

F32 = mybir.dt.float32
BF16 = mybir.dt.bfloat16
I32 = mybir.dt.int32
U32 = mybir.dt.uint32
U16 = mybir.dt.uint16
U8 = mybir.dt.uint8
FP8X4 = mybir.dt.float8_e4m3fn_x4
ALU = mybir.AluOpType
ACT = mybir.ActivationFunctionType

P = 128
PACK = 4
T = 2048
S = 512
HALF = S // 2
RUNS = 16
SCORE_SCALE = 0.0625
FLOPS = 3 * 2 * 512 * 512 * 512


def entries(lst, start, count):
    return lst[:, start // 16 : (start + count) // 16]


def flat(pair):
    return pair.rearrange("p i n -> p (i n)")


def tile_picked_ccmpsoftbtop2_none_p_kernel(
    tc, x_words, x_scales, w1, gs, offs, n1, n2, n3, ca, cb, n4, n5, out
):
    nc = tc.nc
    with ExitStack() as ctx:
        keep = ctx.enter_context(tc.tile_pool(name="keep", bufs=1))
        psum = ctx.enter_context(tc.psum_pool(name="psum", bufs=1))

        def bank(index):
            return psum.tile([P, S], F32, name="bank", tag="bank%d" % index)

        def load_list(name, src):
            lst = keep.tile([P, S // 16], U16, name=name)
            nc.sync.dma_start(lst[:], src)
            return lst

        table_scales = keep.tile([P, T], U8, name="table_scales")
        nc.vector.memset(table_scales[:].bitcast(I32), 0)
        ident = keep.tile([P, P], F32, name="ident")
        make_identity(nc, ident[:])

        l_offs = load_list("l_offs", offs)
        l_cb = load_list("l_cb", cb)
        for q in range(4):
            nc.sync.dma_start(
                table_scales[32 * q : 32 * q + 4, :].bitcast(I32),
                x_scales[0, 4 * q : 4 * q + 4, :].bitcast(I32),
            )
        halves = (slice(0, HALF), slice(HALF, S))
        w_view = w1.rearrange("(p j) c -> p j c", j=PACK)
        w_raw = [keep.tile([P, PACK, HALF], F32, name="w_raw%d" % h) for h in range(2)]
        for h in range(2):
            nc.sync.dma_start(w_raw[h][:], w_view[:, :, halves[h]])
        l_ca = load_list("l_ca", ca)
        table_words = keep.tile([P, T], I32, name="table_words")
        nc.sync.dma_start(table_words[:], x_words[0].rearrange("p n r -> p (n r)").bitcast(I32))
        l_n1 = load_list("l_n1", n1)
        l_n2 = load_list("l_n2", n2)
        l_n3 = load_list("l_n3", n3)
        gs_sb = keep.tile([P, PACK], F32, name="gs_sb")
        nc.sync.dma_start(gs_sb[:], gs.rearrange("(p t) o -> p (t o)", t=PACK))
        l_n5 = load_list("l_n5", n5)
        l_n4 = load_list("l_n4", n4)
        words_window = table_words[:].bitcast(U32)

        xq_scales = keep.tile([P, S], U8, name="xq_scales", align_bytes=64)
        nc.vector.tensor_copy(xq_scales[:], table_scales[:].indirect(l_offs[:]))
        listed_scales = keep.tile([P, 2 * S], U8, name="listed_scales", align_bytes=64)
        nc.vector.tensor_copy(listed_scales[:, 0:S], table_scales[:].indirect(l_cb[:]))
        nc.vector.tensor_copy(listed_scales[:, S : 2 * S], table_scales[:].indirect(l_ca[:]))

        w_bf = keep.tile([P, PACK, P, PACK], BF16, name="w_bf", align_bytes=64)
        for h in range(2):
            nc.scalar.copy(
                w_bf[:, :, P // 2 * h : P // 2 * (h + 1), :].rearrange("p t m j -> p m j t"),
                w_raw[h][:].rearrange("p j (m t) -> p m j t", t=PACK),
            )
        w_codes = keep.tile([P, S], U32, name="w_codes", align_bytes=64)
        w_scales = keep.tile([P, S], U8, name="w_scales", align_bytes=64)
        nc.vector.quantize_mx(w_codes[:].bitcast(FP8X4), w_scales[:], w_bf[:].rearrange("p t m j -> p (t m j)"))

        xq_words = keep.tile([P, S], U32, name="xq_words", align_bytes=64)
        for j0 in (0, HALF):
            nc.vector.tensor_copy(xq_words[:, j0 : j0 + HALF], words_window.indirect(entries(l_offs, j0, HALF)))

        pair_scales = keep.tile([P, 2 * S], U8, name="pair_scales", align_bytes=64)
        nc.vector.tensor_copy(
            pair_scales[:].bitcast(I32).rearrange("p (l t g r) -> p l t g r", l=2, t=PACK, g=RUNS),
            listed_scales[:].bitcast(I32).rearrange("p (l g t r) -> p l t g r", l=2, t=PACK, g=RUNS),
        )
        cb_scales, ca_scales = pair_scales[:, 0:S], pair_scales[:, S : 2 * S]

        def gather_dealt_words(words, lst):
            nc.vector.tensor_copy(
                words[:].rearrange("p (t g r) -> p g t r", t=PACK, g=RUNS), words_window.indirect(lst[:])
            )

        cb_words = keep.tile([P, S], U32, name="cb_words", align_bytes=64)
        gather_dealt_words(cb_words, l_cb)

        def product(acc, stationary_words, stationary_scales, t, moving_words, moving_scales):
            cols = slice(P * t, P * (t + 1))
            nc.tensor.matmul_mx(
                acc, stationary_words[:, cols].bitcast(FP8X4), stationary_scales[:, cols],
                moving_words.bitcast(FP8X4), moving_scales, start=True, stop=True,
            )

        half_y = [keep.tile([P, S], F32, name="half_y%d" % t) for t in range(PACK)]

        def project(acc, t, js):
            product(acc[:, js], w_codes, w_scales, t, xq_words[:, js], xq_scales[:, js])
            nc.scalar.activation(half_y[t][:, js], acc[:, js], ACT.Copy, scale=0.5)

        for first_bank, js in zip((0, PACK), halves):
            for t in range(2):
                project(bank(first_bank + t), t, js)
        for t in range(2, PACK):
            project(bank(t), t, slice(0, S))

        z_codes = keep.tile([P, S], U32, name="z_codes", align_bytes=64)
        z_scales = keep.tile([P, S], U8, name="z_scales", align_bytes=64)
        b_rows = [keep.tile([P, 2 * S], F32, name="b_rows%d" % t, align_bytes=64) for t in range(PACK)]
        a_rows = [keep.tile([P, 2 * S], F32, name="a_rows%d" % t, align_bytes=64) for t in range(PACK)]
        b_tanh = [keep.tile([P, S], F32, name="b_tanh%d" % t) for t in range(PACK)]
        z_planes = [
            keep.tile([P, 2, PACK, P], BF16, name="z_planes", tag="z_planes%d" % c, align_bytes=64) for c in range(2)
        ]
        neg_gs = keep.tile([P, PACK], F32, name="neg_gs")
        nc.scalar.activation(neg_gs[:], gs_sb[:], ACT.Copy, scale=-1.0)

        def pair_tile(name, tag):
            return keep.tile([P, 2, HALF], F32, name=name, tag=tag, align_bytes=64)[:]

        def weave(j0, width, copy):
            c, off = divmod(j0, HALF)
            z_bf = keep.tile([P, width, PACK], BF16, name="z_bf", tag="z_bf%d" % j0, align_bytes=64)
            copy(
                z_bf[:].rearrange("p (s c i) t -> p s c t i", i=4, c=P // 4),
                z_planes[c][:, off // P : (off + width) // P].rearrange("p s t (c i) -> p s c t i", i=4),
            )
            return z_bf

        def quantize(z_bf, j0, width):
            js = slice(j0, j0 + width)
            nc.vector.quantize_mx(z_codes[:, js].bitcast(FP8X4), z_scales[:, js], z_bf[:].rearrange("p n t -> p (n t)"))

        def score_b(acc, t, j0, width):
            js = slice(j0, j0 + width)
            product(acc[:, js], cb_words, cb_scales, t, z_codes[:, js], z_scales[:, js])
            nc.scalar.activation(b_rows[t][:, js], acc[:, js], ACT.Copy, scale=SCORE_SCALE)

        def tanh_b(acc, t, j0, width):
            js = slice(j0, j0 + width)
            nc.scalar.activation(b_tanh[t][:, js], acc[:, js], ACT.Tanh, scale=SCORE_SCALE)

        def add_turned(acc, terms, blocks):
            for blk in blocks:
                cols = slice(P * blk, P * (blk + 1))
                for i, term in enumerate(terms):
                    nc.tensor.matmul(
                        acc[:, cols], term[:, cols], ident[:],
                        start=(i == 0), stop=(i == len(terms) - 1), is_transpose=True,
                    )

        def look_up(quarter, h1_tag, gap_tag, third, third_op):
            c, u = divmod(quarter, 2)
            j0 = c * HALF
            h1 = pair_tile("h1", h1_tag)
            d = pair_tile("d", "d%d" % quarter)
            gap = pair_tile("gap", gap_tag)
            hi = a_rows[quarter][:, S:].rearrange("p (i n) -> p i n", i=2)
            e = b_rows[quarter][:, S:].rearrange("p (i n) -> p i n", i=2)
            for i in range(2):
                nc.vector.tensor_copy(h1[:, i, :], half_y[2 * u + i][:].indirect(entries(l_n1, j0, HALF)))
            for i in range(2):
                nc.vector.tensor_tensor(
                    d[:, i, :], half_y[2 * u + i][:].indirect(entries(l_n2, j0, HALF)), h1[:, i, :], ALU.subtract
                )
            nc.scalar.activation(flat(gap), flat(d), ACT.Abs)
            for i in range(2):
                nc.vector.scalar_tensor_tensor(hi[:, i, :], d[:, i, :], 0.0, h1[:, i, :], ALU.max, ALU.add)
            for i in range(2):
                nc.vector.tensor_tensor(
                    e[:, i, :], third[2 * u + i][:].indirect(entries(l_n3, j0, HALF)), hi[:, i, :], third_op
                )
            return hi, gap, e

        def sum_into_planes(quarter, terms, sign, others, weight):
            c, u = divmod(quarter, 2)
            turned = keep.tile([P, S], F32, name="turned", tag="turned%d" % quarter, align_bytes=64)
            for i in range(2):
                acc = bank((0, 7)[i])
                add_turned(acc, terms, (2 * i, 2 * i + 1))
                nc.scalar.activation(turned[:, halves[i]], acc[:, halves[i]], ACT.Copy, scale=sign)
            for i in range(2):
                t = 2 * u + i
                acc = bank((1, 3)[i])
                add_turned(acc, [turned[:]] + others, (2 * i, 2 * i + 1))
                nc.scalar.activation(
                    z_planes[c][:, :, t, :], acc[:, halves[i]].rearrange("p (s j) -> p s j", j=P),
                    ACT.Copy, scale=weight[:, t : t + 1],
                )

        neg_y = [keep.tile([P, S], F32, name="neg_y%d" % t) for t in range(2)]
        for quarter in range(2):
            hi, gap, e = look_up(quarter, "h1", "gap%d" % quarter, half_y, ALU.subtract)
            rise = pair_tile("rise", "rise")
            for i in range(2):
                nc.scalar.activation(rise[:, i, :], e[:, i, :], ACT.Relu, scale=3.0)
            acc = bank(6)
            add_turned(acc, [flat(e), flat(gap)], range(PACK))
            clip = keep.tile([P, S], F32, name="clip%d" % quarter, align_bytes=64)
            nc.scalar.activation(clip[:], acc[:], ACT.Relu)
            sum_into_planes(quarter, [flat(rise), flat(hi), flat(gap)], -1.0, [clip[:]], neg_gs)
            if quarter == 0:
                for t in range(2):
                    nc.scalar.activation(neg_y[t][:], half_y[t][:], ACT.Copy, scale=-1.0)
        quantize(weave(0, HALF, nc.scalar.copy), 0, HALF)

        hi, gap, neg_e = look_up(2, "h1", "gap0", neg_y, ALU.add)
        low = pair_tile("low", "low2")
        for i in range(2):
            nc.vector.scalar_tensor_tensor(low[:, i, :], neg_e[:, i, :], 0.0, gap[:, i, :], ALU.max, ALU.min)
        rise = pair_tile("rise", "gap1")
        for i in range(2):
            nc.scalar.activation(rise[:, i, :], neg_e[:, i, :], ACT.Relu, scale=-2.0)
        sum_into_planes(2, [flat(low), flat(hi), flat(rise)], 1.0, [], gs_sb)
        acc = bank(1)
        score_b(acc, 0, 0, HALF)
        tanh_b(acc, 0, 0, HALF)

        hi, gap, e = look_up(3, "gap0", "z_planes0", half_y, ALU.subtract)
        weighted_hi = pair_tile("weighted_hi", "turned2")
        for i in range(2):
            nc.scalar.activation(weighted_hi[:, i, :], hi[:, i, :], ACT.Copy, scale=gs_sb[:, 2 + i : 3 + i])
        low = pair_tile("low", "low3")
        for i in range(2):
            nc.vector.scalar_tensor_tensor(low[:, i, :], e[:, i, :], -1.0, gap[:, i, :], ALU.mult, ALU.min)
        top = pair_tile("top", "top")
        for i in range(2):
            nc.vector.scalar_tensor_tensor(top[:, i, :], e[:, i, :], 2.0, low[:, i, :], ALU.mult, ALU.max)
        for s in range(2):
            js = slice(P * s, P * (s + 1))
            for i in range(2):
                nc.vector.scalar_tensor_tensor(
                    z_planes[1][:, s, 2 + i, :], top[:, i, js], gs_sb[:, 2 + i : 3 + i], weighted_hi[:, i, js],
                    ALU.mult, ALU.add,
                )

        starts = (HALF, HALF + P)
        woven = [weave(j0, P, nc.vector.tensor_copy) for j0 in starts]
        accs = [bank(2), bank(PACK)]
        for z_bf, j0, acc in zip(woven, starts, accs):
            quantize(z_bf, j0, P)
            score_b(acc, 0, j0, P)
        for j0, acc in zip(starts, accs):
            tanh_b(acc, 0, j0, P)

        ca_words = keep.tile([P, S], U32, name="ca_words", tag="z_bf%d" % HALF, align_bytes=64)
        gather_dealt_words(ca_words, l_ca)

        def score_a(t):
            acc = bank(t)
            product(acc[:], ca_words, ca_scales, t, z_codes[:], z_scales[:])
            nc.scalar.activation(a_rows[t][:, 0:S], acc[:], ACT.Copy, scale=SCORE_SCALE)

        for t in range(1, PACK):
            acc = bank(PACK + t)
            score_b(acc, t, 0, S)
            tanh_b(acc, t, 0, S)
            score_a(t - 1)
        score_a(PACK - 1)

        out_view = out.rearrange("(g t r) j -> t g r j", t=PACK, g=RUNS)
        prod = [keep.tile([P, S], F32, name="prod%d" % t) for t in range(PACK)]
        res = [keep.tile([P, S], F32, name="res%d" % t) for t in range(PACK)]
        whole, halved = ((0, S),), ((0, HALF), (HALF, HALF))

        def times_tanh(t):
            for j0, width in halved if t == 0 else whole:
                js = slice(j0, j0 + width)
                nc.vector.tensor_tensor(
                    prod[t][:, js], b_rows[t][:].indirect(entries(l_n5, j0, width)), b_tanh[t][:, js], ALU.mult
                )

        def result(t):
            for j0, width in halved if t == PACK - 1 else whole:
                js = slice(j0, j0 + width)
                nc.vector.tensor_tensor(
                    res[t][:, js], a_rows[t][:].indirect(entries(l_n4, j0, width)), prod[t][:, js], ALU.subtract
                )
                nc.sync.dma_start(out_view[t, :, :, js], res[t][:, js])

        times_tanh(0)
        for t in range(1, PACK):
            times_tanh(t)
            result(t - 1)
        result(PACK - 1)
